import numpy as np
import ml_dtypes


def mxq(x, axis, fmt="e4m3"):
    dtype, down = {"e4m3": (ml_dtypes.float8_e4m3fn, 7), "e5m2": (ml_dtypes.float8_e5m2, 14)}[fmt]
    v = np.moveaxis(np.asarray(x, np.float32).astype(ml_dtypes.bfloat16).astype(np.float64), axis, -1)
    blocks = v.reshape(v.shape[:-1] + (-1, 32))
    amax = np.abs(blocks).max(-1, keepdims=True)
    byte = np.maximum(np.where(amax > 0, np.frexp(amax)[1] - 1 + 127, 0) - down, 1)
    scale = np.exp2(byte - 127.0)
    codes = (blocks / scale).astype(np.float32).astype(dtype).astype(np.float64)
    return np.moveaxis((codes * scale).reshape(v.shape), -1, axis)


WIDE = False


def mx_kscale(k):
    if not WIDE:
        return np.ones(k)
    levels = np.array([30, -30])
    if k % 512:
        return np.exp2(np.random.permutation(np.resize(levels, k // 32))).repeat(32)
    a = np.empty((k // 512, 16))
    for p in range(k // 512):
        a[p, :8] = np.random.permutation(np.resize(levels, 8))
        for g in range(8):
            far = levels[np.abs(levels - a[p, g]) >= 10]
            a[p, g + 8] = far[np.random.randint(len(far))]
    return np.exp2(a.ravel()).repeat(32)


def f64(x):
    return np.asarray(x).astype(np.float64)


def striped(idx):
    return np.tile(np.asarray(idx).reshape(-1, 16).T, (8, 1)).astype(np.uint16)


def unstriped(offs):
    return offs[:16].T.reshape(-1).astype(np.int64)


def bf(x):
    return np.asarray(x, np.float32).astype(ml_dtypes.bfloat16)


def planes(Y):
    r, m = Y.shape
    b = f64(bf(Y)).reshape(r // 32, 32, m)
    amax = np.abs(b).max(1)
    byte = np.clip(np.where(amax > 0, np.frexp(amax)[1] - 1 + 127 - 7, 1), 1, 254)
    codes = (b * np.exp2(127.0 - byte)[:, None, :]).reshape(r, m).astype(np.float32).astype(ml_dtypes.float8_e4m3fn).view(np.uint8)
    words = codes.reshape(r // 512, 128, 4, m).transpose(0, 1, 3, 2)
    return np.ascontiguousarray(words), np.ascontiguousarray(byte.astype(np.uint8).reshape(r // 512, 16, m))


T, K, N, J = 1024, 512, 1024, 512


def setup_inputs():
    n = np.random.standard_normal
    idx = np.random.permutation(N)[:J]
    ft = mx_kscale(T)
    return {
        "xt": (n((T, K)) * ft[:, None]).astype(np.float32),
        "g": (n((T, N)) * np.exp(0.5 * n((T, 1))) / ft[:, None]).astype(np.float32),
        "mom": (1.0 * n((K, N))).astype(np.float32),
        "offs": striped(idx),
    }


def reference(xt, g, mom, offs):
    idx = unstriped(offs)
    xtq = mxq(f64(xt), 0, "e4m3")
    gidxq = mxq(f64(g)[:, idx], 0, "e5m2")
    w = xtq.T @ gidxq
    d = 0.03 * w - 0.1 * f64(mom)[:, idx]
    p = np.zeros((K, N))
    p[:, idx] = d
    y = f64(mom) + p
    words, scales = planes(y)
    return y, words, scales

@@ -1,0 +1,169 @@
+from contextlib import ExitStack
+
+import concourse.mybir as mybir
+
+T, K, N, J = 1024, 512, 1024, 512
+FLOPS = 2 * T * K * J
+
+F32 = mybir.dt.float32
+BF16 = mybir.dt.bfloat16
+U32 = mybir.dt.uint32
+I32 = mybir.dt.int32
+U16 = mybir.dt.uint16
+U8 = mybir.dt.uint8
+E4M3 = mybir.dt.float8_e4m3fn_x4
+E5M2 = mybir.dt.float8_e5m2_x4
+ALU = mybir.AluOpType
+COPY = mybir.ActivationFunctionType.Copy
+
+P = 128
+PACK = 4
+T_PASS = P * PACK
+PASSES = T // T_PASS
+HALF = J // 2
+LIST_COLS = HALF // 16
+CHUNK = 256
+
+
+def tile_list_sparse_momentum_pl_kernel(tc, xt, g, mom, offs, out_0, out_1, out_2):
+    nc = tc.nc
+    with ExitStack() as ctx:
+        sb = ctx.enter_context(tc.tile_pool(name="sb", bufs=1))
+        psum = ctx.enter_context(tc.psum_pool(name="psum", bufs=1))
+
+        def tile(shape, dtype, name):
+            return sb.tile(shape, dtype, name=name, align_bytes=64)
+
+        offsets = sb.tile([P, J // 16], U16, name="offsets")
+        nc.sync.dma_start(offsets[:], offs)
+
+        def listed(h):
+            return offsets[:, h * LIST_COLS : (h + 1) * LIST_COLS]
+
+        g_rows = g.rearrange("(a p i) n -> a i p n", p=P, i=PACK)
+        x_rows = xt.rearrange("(a p i) k -> a p i k", p=P, i=PACK)
+        g_raw, x_raw = {}, {}
+        for a in range(PASSES):
+            for i in range(PACK):
+                g_raw[a, i] = tile([P, N], F32, f"g_raw{a}{i}")
+                nc.sync.dma_start(g_raw[a, i][:], g_rows[a, i])
+            x_raw[a] = tile([P, PACK, K], F32, f"x_raw{a}")
+            nc.sync.dma_start(x_raw[a][:], x_rows[a])
+        mom_rows = mom.rearrange("(p r) n -> r p n", r=PACK)
+        mom0 = tile([P, N], F32, "mom0")
+        mom1 = tile([P, N], F32, "mom1")
+        mom32 = tile([P, 2 * N], F32, "mom32")
+        m_rows = [mom0[:], mom1[:], mom32[:, N : 2 * N], mom32[:, 0:N]]
+        for r in range(PACK):
+            nc.sync.dma_start(m_rows[r], mom_rows[r])
+
+        pages = [tile([P, N], F32, f"page{r}") for r in range(PACK)]
+        for r in range(PACK):
+            nc.gpsimd.memset(pages[r][:], 0.0)
+
+        acc = {(r, h): psum.tile([P, HALF], F32, name=f"acc{r}{h}") for r in range(PACK) for h in range(2)}
+        for a in range(PASSES):
+            picked = [tile([P, PACK, HALF], BF16, f"picked{a}{h}") for h in range(2)]
+            for i in range(PACK):
+                nc.scalar.activation(out=picked[0][:, i, :], in_=g_raw[a, i][:].indirect(listed(0)), func=COPY)
+                nc.vector.tensor_copy(out=picked[1][:, i, :], in_=g_raw[a, i][:].indirect(listed(1)))
+            g_codes, g_scales = {}, {}
+            for h, copy in ((1, nc.vector.tensor_copy), (0, nc.scalar.copy)):
+                woven = tile([P, HALF, PACK], BF16, f"g_woven{a}{h}")
+                copy(
+                    out=woven[:].rearrange("p (c e) i -> p c i e", e=4),
+                    in_=picked[h][:].rearrange("p i (c e) -> p c i e", e=4),
+                )
+                g_codes[h] = tile([P, HALF], U32, f"g_codes{a}{h}")
+                g_scales[h] = tile([P, HALF], U8, f"g_scales{a}{h}")
+                nc.vector.quantize_mx(
+                    out=g_codes[h][:].bitcast(E5M2), scales=g_scales[h][:], in_=woven[:].rearrange("p c i -> p (c i)")
+                )
+            for q in range(2):
+                woven = tile([P, 2, P, PACK], BF16, "x_woven")
+                nc.vector.tensor_copy(
+                    out=woven[:].rearrange("p s m i -> p m i s"),
+                    in_=x_raw[a][:].rearrange("p i (m r) -> p m i r", r=PACK)[:, :, :, 2 * q : 2 * q + 2],
+                )
+                for s in range(2):
+                    r = 2 * q + s
+                    codes = tile([P, P], U32, f"x_codes{a}{r}")
+                    scales = tile([P, P], U8, f"x_scales{a}{r}")
+                    nc.vector.quantize_mx(
+                        out=codes[:].bitcast(E4M3),
+                        scales=scales[:],
+                        in_=woven[:, s, :, :].rearrange("p m i -> p (m i)"),
+                    )
+                    for h in range(2):
+                        nc.tensor.matmul_mx(
+                            out=acc[r, h][:],
+                            lhsT=codes[:].bitcast(E4M3),
+                            lhsT_scale=scales[:],
+                            rhs=g_codes[h][:].bitcast(E5M2),
+                            rhs_scale=g_scales[h][:],
+                            start=(a == 0),
+                            stop=(a == PASSES - 1),
+                        )
+
+        y = tile([P, PACK * N], F32, "y")
+        y_plane = [y[:, r * N : (r + 1) * N] for r in range(PACK)]
+        y_rows = out_0.rearrange("(p r) n -> r p n", r=PACK)
+        for r in range(PACK):
+            m_picked = tile([P, J], F32, f"m_picked{r}")[:]
+            if r < 3:
+                d = tile([P, J], F32, f"d{r}")[:]
+            else:
+                d = y_plane[2][:, CHUNK // 2 : CHUNK // 2 + J]
+            if r == 3:
+                nc.vector.tensor_scalar(
+                    out=m_picked, in0=mom32[:].indirect(offsets[:]), scalar1=-0.1, scalar2=0.0,
+                    op0=ALU.mult, op1=ALU.add,
+                )
+            for h in range(2):
+                cols = slice(h * HALF, (h + 1) * HALF)
+                if r == 0:
+                    nc.scalar.activation(out=m_picked[:, cols], in_=m_rows[r].indirect(listed(h)), func=COPY)
+                elif r < 3:
+                    nc.vector.tensor_copy(out=m_picked[:, cols], in_=m_rows[r].indirect(listed(h)))
+            for h in range(2):
+                cols = slice(h * HALF, (h + 1) * HALF)
+                nc.vector.scalar_tensor_tensor(
+                    out=d[:, cols], in0=acc[r, h][:], scalar=(0.03 if r == 3 else -0.3), in1=m_picked[:, cols],
+                    op0=ALU.mult, op1=ALU.add,
+                )
+                if r < 3:
+                    nc.scalar.activation(out=pages[r][:].indirect(listed(h)), in_=d[:, cols], func=COPY, scale=-0.1)
+            if r == 3:
+                nc.vector.tensor_copy(out=pages[r][:].indirect(offsets[:]), in_=d)
+
+        for r in (0, 1):
+            nc.gpsimd.tensor_tensor(out=y_plane[r], in0=m_rows[r], in1=pages[r][:], op=ALU.add)
+            nc.sync.dma_start(y_rows[r], y_plane[r])
+        nc.vector.tensor_tensor(out=y_plane[3], in0=m_rows[3], in1=pages[3][:], op=ALU.add)
+        nc.sync.dma_start(y_rows[3], y_plane[3])
+        for cols in (slice(0, CHUNK), slice(CHUNK, 2 * CHUNK), slice(2 * CHUNK, N)):
+            nc.vector.tensor_tensor(out=y_plane[2][:, cols], in0=m_rows[2][:, cols], in1=pages[2][:, cols], op=ALU.add)
+        nc.sync.dma_start(y_rows[2], y_plane[2])
+
+        y_scales = tile([P, N], U8, "y_scales")
+        words = out_1.rearrange("z p c r -> p (z c r)").bitcast(I32)
+        y_woven = [tile([P, CHUNK, PACK], BF16, f"y_woven{c}") for c in range(N // CHUNK)]
+        for c in (0, 2, 1, 3):
+            cols = slice(c * CHUNK, (c + 1) * CHUNK)
+            dst = y_woven[c][:].rearrange("p (c e) r -> p c r e", e=4)
+            src = y[:].rearrange("p (r n) -> p r n", r=PACK)[:, :, cols].rearrange("p r (c e) -> p c r e", e=4)
+            if c < 2:
+                nc.scalar.copy(out=dst, in_=src)
+            else:
+                nc.vector.tensor_copy(out=dst, in_=src)
+        for c in (0, 2, 1, 3):
+            cols = slice(c * CHUNK, (c + 1) * CHUNK)
+            y_codes = tile([P, CHUNK], U32, f"y_codes{c}")
+            nc.vector.quantize_mx(
+                out=y_codes[:].bitcast(E4M3), scales=y_scales[:, cols], in_=y_woven[c][:].rearrange("p c r -> p (c r)")
+            )
+            nc.sync.dma_start(words[:, cols], y_codes[:].bitcast(I32))
+        scale_rows = out_2.rearrange("z q c -> (z q) c").bitcast(I32)
+        for q in range(4):
+            queue = nc.scalar if q % 2 == 0 else nc.sync
+            queue.dma_start(scale_rows[4 * q : 4 * q + 4, :], y_scales[32 * q : 32 * q + 4, :].bitcast(I32))

@@ -23,6 +23,7 @@ PASSES = T // T_PASS
 HALF = J // 2
 LIST_COLS = HALF // 16
 CHUNK = 256
+SPLIT = 384
 
 
 def tile_list_sparse_momentum_pl_kernel(tc, xt, g, mom, offs, out_0, out_1, out_2):
@@ -61,27 +62,30 @@ def tile_list_sparse_momentum_pl_kernel(tc, xt, g, mom, offs, out_0, out_1, out_
         for r in range(PACK):
             nc.gpsimd.memset(pages[r][:], 0.0)
 
-        acc = {(r, h): psum.tile([P, HALF], F32, name=f"acc{r}{h}") for r in range(PACK) for h in range(2)}
+        halves = [slice(h * HALF, (h + 1) * HALF) for h in range(2)]
+        sums = [(0, halves[0]), (0, halves[1])] + [(r, slice(0, J)) for r in range(1, PACK)]
+        acc = {(r, js.start): psum.tile([P, js.stop - js.start], F32, name=f"acc{r}_{js.start}") for r, js in sums}
         for a in range(PASSES):
             picked = [tile([P, PACK, HALF], BF16, f"picked{a}{h}") for h in range(2)]
             for i in range(PACK):
                 nc.scalar.activation(out=picked[0][:, i, :], in_=g_raw[a, i][:].indirect(listed(0)), func=COPY)
                 nc.vector.tensor_copy(out=picked[1][:, i, :], in_=g_raw[a, i][:].indirect(listed(1)))
-            g_codes, g_scales = {}, {}
+            g_codes = tile([P, J], U32, f"g_codes{a}")
+            g_scales = tile([P, J], U8, f"g_scales{a}")
             for h, copy in ((1, nc.vector.tensor_copy), (0, nc.scalar.copy)):
                 woven = tile([P, HALF, PACK], BF16, f"g_woven{a}{h}")
                 copy(
                     out=woven[:].rearrange("p (c e) i -> p c i e", e=4),
                     in_=picked[h][:].rearrange("p i (c e) -> p c i e", e=4),
                 )
-                g_codes[h] = tile([P, HALF], U32, f"g_codes{a}{h}")
-                g_scales[h] = tile([P, HALF], U8, f"g_scales{a}{h}")
                 nc.vector.quantize_mx(
-                    out=g_codes[h][:].bitcast(E5M2), scales=g_scales[h][:], in_=woven[:].rearrange("p c i -> p (c i)")
+                    out=g_codes[:, halves[h]].bitcast(E5M2),
+                    scales=g_scales[:, halves[h]],
+                    in_=woven[:].rearrange("p c i -> p (c i)"),
                 )
-            for q in range(2):
-                woven = tile([P, 2, P, PACK], BF16, "x_woven")
-                nc.vector.tensor_copy(
+            for q, copy in ((0, nc.vector.tensor_copy), (1, nc.scalar.copy)):
+                woven = tile([P, 2, P, PACK], BF16, f"x_woven{a}{q}")
+                copy(
                     out=woven[:].rearrange("p s m i -> p m i s"),
                     in_=x_raw[a][:].rearrange("p i (m r) -> p m i r", r=PACK)[:, :, :, 2 * q : 2 * q + 2],
                 )
@@ -94,13 +98,13 @@ def tile_list_sparse_momentum_pl_kernel(tc, xt, g, mom, offs, out_0, out_1, out_
                         scales=scales[:],
                         in_=woven[:, s, :, :].rearrange("p m i -> p (m i)"),
                     )
-                    for h in range(2):
+                    for js in [js for plane, js in sums if plane == r]:
                         nc.tensor.matmul_mx(
-                            out=acc[r, h][:],
+                            out=acc[r, js.start][:],
                             lhsT=codes[:].bitcast(E4M3),
                             lhsT_scale=scales[:],
-                            rhs=g_codes[h][:].bitcast(E5M2),
-                            rhs_scale=g_scales[h][:],
+                            rhs=g_codes[:, js].bitcast(E5M2),
+                            rhs_scale=g_scales[:, js],
                             start=(a == 0),
                             stop=(a == PASSES - 1),
                         )
@@ -108,42 +112,39 @@ def tile_list_sparse_momentum_pl_kernel(tc, xt, g, mom, offs, out_0, out_1, out_
         y = tile([P, PACK * N], F32, "y")
         y_plane = [y[:, r * N : (r + 1) * N] for r in range(PACK)]
         y_rows = out_0.rearrange("(p r) n -> r p n", r=PACK)
-        for r in range(PACK):
-            m_picked = tile([P, J], F32, f"m_picked{r}")[:]
-            if r < 3:
-                d = tile([P, J], F32, f"d{r}")[:]
+        for r in range(3):
+            m_picked = tile([P, J], F32, f"m_picked{r}")
+            d = tile([P, J], F32, f"d{r}")
+            if r == 0:
+                for h in range(2):
+                    nc.scalar.activation(out=m_picked[:, halves[h]], in_=m_rows[r].indirect(listed(h)), func=COPY)
             else:
-                d = y_plane[2][:, CHUNK // 2 : CHUNK // 2 + J]
-            if r == 3:
-                nc.vector.tensor_scalar(
-                    out=m_picked, in0=mom32[:].indirect(offsets[:]), scalar1=-0.1, scalar2=0.0,
-                    op0=ALU.mult, op1=ALU.add,
-                )
-            for h in range(2):
-                cols = slice(h * HALF, (h + 1) * HALF)
-                if r == 0:
-                    nc.scalar.activation(out=m_picked[:, cols], in_=m_rows[r].indirect(listed(h)), func=COPY)
-                elif r < 3:
-                    nc.vector.tensor_copy(out=m_picked[:, cols], in_=m_rows[r].indirect(listed(h)))
-            for h in range(2):
-                cols = slice(h * HALF, (h + 1) * HALF)
+                nc.vector.tensor_copy(out=m_picked[:], in_=m_rows[r].indirect(offsets[:]))
+            for js in [js for plane, js in sums if plane == r]:
                 nc.vector.scalar_tensor_tensor(
-                    out=d[:, cols], in0=acc[r, h][:], scalar=(0.03 if r == 3 else -0.3), in1=m_picked[:, cols],
-                    op0=ALU.mult, op1=ALU.add,
+                    out=d[:, js], in0=acc[r, js.start][:], scalar=-0.3, in1=m_picked[:, js], op0=ALU.mult, op1=ALU.add
                 )
-                if r < 3:
-                    nc.scalar.activation(out=pages[r][:].indirect(listed(h)), in_=d[:, cols], func=COPY, scale=-0.1)
-            if r == 3:
-                nc.vector.tensor_copy(out=pages[r][:].indirect(offsets[:]), in_=d)
+            for h in range(2):
+                nc.scalar.activation(out=pages[r][:].indirect(listed(h)), in_=d[:, halves[h]], func=COPY, scale=-0.1)
+        m_picked = y_plane[0][:, 0:J]
+        nc.vector.tensor_scalar(
+            out=m_picked, in0=mom32[:].indirect(offsets[:]), scalar1=-0.1, scalar2=0.0, op0=ALU.mult, op1=ALU.add
+        )
+        d_scalar = tile([P, J - SPLIT], F32, "d_scalar")
+        d_vector = y[:, 2 * N - SPLIT // 2 : 2 * N + SPLIT // 2]
+        for d, js in ((d_vector, slice(0, SPLIT)), (d_scalar[:], slice(SPLIT, J))):
+            nc.vector.scalar_tensor_tensor(
+                out=d, in0=acc[3, 0][:, js], scalar=0.03, in1=m_picked[:, js], op0=ALU.mult, op1=ALU.add
+            )
+        nc.vector.tensor_copy(out=pages[3][:].indirect(offsets[:, 0 : SPLIT // 16]), in_=d_vector)
+        nc.scalar.activation(out=pages[3][:].indirect(offsets[:, SPLIT // 16 : J // 16]), in_=d_scalar[:], func=COPY)
 
-        for r in (0, 1):
-            nc.gpsimd.tensor_tensor(out=y_plane[r], in0=m_rows[r], in1=pages[r][:], op=ALU.add)
+        for r in range(3):
+            nc.vector.tensor_tensor(out=y_plane[r], in0=m_rows[r], in1=pages[r][:], op=ALU.add)
             nc.sync.dma_start(y_rows[r], y_plane[r])
-        nc.vector.tensor_tensor(out=y_plane[3], in0=m_rows[3], in1=pages[3][:], op=ALU.add)
-        nc.sync.dma_start(y_rows[3], y_plane[3])
         for cols in (slice(0, CHUNK), slice(CHUNK, 2 * CHUNK), slice(2 * CHUNK, N)):
-            nc.vector.tensor_tensor(out=y_plane[2][:, cols], in0=m_rows[2][:, cols], in1=pages[2][:, cols], op=ALU.add)
-        nc.sync.dma_start(y_rows[2], y_plane[2])
+            nc.vector.tensor_tensor(out=y_plane[3][:, cols], in0=m_rows[3][:, cols], in1=pages[3][:, cols], op=ALU.add)
+        nc.sync.dma_start(y_rows[3], y_plane[3])
 
         y_scales = tile([P, N], U8, "y_scales")
         words = out_1.rearrange("z p c r -> p (z c r)").bitcast(I32)

@@ -23,7 +23,6 @@ PASSES = T // T_PASS
 HALF = J // 2
 LIST_COLS = HALF // 16
 CHUNK = 256
-SPLIT = 384
 
 
 def tile_list_sparse_momentum_pl_kernel(tc, xt, g, mom, offs, out_0, out_1, out_2):
@@ -53,10 +52,11 @@ def tile_list_sparse_momentum_pl_kernel(tc, xt, g, mom, offs, out_0, out_1, out_
         mom_rows = mom.rearrange("(p r) n -> r p n", r=PACK)
         mom0 = tile([P, N], F32, "mom0")
         mom1 = tile([P, N], F32, "mom1")
-        mom32 = tile([P, 2 * N], F32, "mom32")
-        m_rows = [mom0[:], mom1[:], mom32[:, N : 2 * N], mom32[:, 0:N]]
-        for r in range(PACK):
+        mom23 = tile([P, 2 * N], F32, "mom23")
+        m_rows = [mom0[:], mom1[:], mom23[:, 0:N], mom23[:, N : 2 * N]]
+        for r in range(2):
             nc.sync.dma_start(m_rows[r], mom_rows[r])
+        nc.sync.dma_start(mom23[:], mom.rearrange("(p u e) n -> u p (e n)", u=2, e=2)[1])
 
         pages = [tile([P, N], F32, f"page{r}") for r in range(PACK)]
         for r in range(PACK):
@@ -65,13 +65,14 @@ def tile_list_sparse_momentum_pl_kernel(tc, xt, g, mom, offs, out_0, out_1, out_
         halves = [slice(h * HALF, (h + 1) * HALF) for h in range(2)]
         sums = [(0, halves[0]), (0, halves[1])] + [(r, slice(0, J)) for r in range(1, PACK)]
         acc = {(r, js.start): psum.tile([P, js.stop - js.start], F32, name=f"acc{r}_{js.start}") for r, js in sums}
+        g_codes, g_scales = {}, {}
         for a in range(PASSES):
             picked = [tile([P, PACK, HALF], BF16, f"picked{a}{h}") for h in range(2)]
             for i in range(PACK):
                 nc.scalar.activation(out=picked[0][:, i, :], in_=g_raw[a, i][:].indirect(listed(0)), func=COPY)
                 nc.vector.tensor_copy(out=picked[1][:, i, :], in_=g_raw[a, i][:].indirect(listed(1)))
-            g_codes = tile([P, J], U32, f"g_codes{a}")
-            g_scales = tile([P, J], U8, f"g_scales{a}")
+            g_codes[a] = tile([P, J], U32, f"g_codes{a}")
+            g_scales[a] = tile([P, J], U8, f"g_scales{a}")
             for h, copy in ((1, nc.vector.tensor_copy), (0, nc.scalar.copy)):
                 woven = tile([P, HALF, PACK], BF16, f"g_woven{a}{h}")
                 copy(
@@ -79,16 +80,17 @@ def tile_list_sparse_momentum_pl_kernel(tc, xt, g, mom, offs, out_0, out_1, out_
                     in_=picked[h][:].rearrange("p i (c e) -> p c i e", e=4),
                 )
                 nc.vector.quantize_mx(
-                    out=g_codes[:, halves[h]].bitcast(E5M2),
-                    scales=g_scales[:, halves[h]],
+                    out=g_codes[a][:, halves[h]].bitcast(E5M2),
+                    scales=g_scales[a][:, halves[h]],
                     in_=woven[:].rearrange("p c i -> p (c i)"),
                 )
-            for q, copy in ((0, nc.vector.tensor_copy), (1, nc.scalar.copy)):
+            for q in range(2):
                 woven = tile([P, 2, P, PACK], BF16, f"x_woven{a}{q}")
-                copy(
-                    out=woven[:].rearrange("p s m i -> p m i s"),
-                    in_=x_raw[a][:].rearrange("p i (m r) -> p m i r", r=PACK)[:, :, :, 2 * q : 2 * q + 2],
-                )
+                for ms, copy in ((slice(0, P // 2), nc.vector.tensor_copy), (slice(P // 2, P), nc.scalar.copy)):
+                    copy(
+                        out=woven[:, :, ms, :].rearrange("p s m i -> p m i s"),
+                        in_=x_raw[a][:].rearrange("p i (m r) -> p m i r", r=PACK)[:, ms, :, 2 * q : 2 * q + 2],
+                    )
                 for s in range(2):
                     r = 2 * q + s
                     codes = tile([P, P], U32, f"x_codes{a}{r}")
@@ -103,8 +105,8 @@ def tile_list_sparse_momentum_pl_kernel(tc, xt, g, mom, offs, out_0, out_1, out_
                             out=acc[r, js.start][:],
                             lhsT=codes[:].bitcast(E4M3),
                             lhsT_scale=scales[:],
-                            rhs=g_codes[:, js].bitcast(E5M2),
-                            rhs_scale=g_scales[:, js],
+                            rhs=g_codes[a][:, js].bitcast(E5M2),
+                            rhs_scale=g_scales[a][:, js],
                             start=(a == 0),
                             stop=(a == PASSES - 1),
                         )
@@ -112,58 +114,75 @@ def tile_list_sparse_momentum_pl_kernel(tc, xt, g, mom, offs, out_0, out_1, out_
         y = tile([P, PACK * N], F32, "y")
         y_plane = [y[:, r * N : (r + 1) * N] for r in range(PACK)]
         y_rows = out_0.rearrange("(p r) n -> r p n", r=PACK)
-        for r in range(3):
-            m_picked = tile([P, J], F32, f"m_picked{r}")
-            d = tile([P, J], F32, f"d{r}")
-            if r == 0:
-                for h in range(2):
-                    nc.scalar.activation(out=m_picked[:, halves[h]], in_=m_rows[r].indirect(listed(h)), func=COPY)
-            else:
-                nc.vector.tensor_copy(out=m_picked[:], in_=m_rows[r].indirect(offsets[:]))
-            for js in [js for plane, js in sums if plane == r]:
-                nc.vector.scalar_tensor_tensor(
-                    out=d[:, js], in0=acc[r, js.start][:], scalar=-0.3, in1=m_picked[:, js], op0=ALU.mult, op1=ALU.add
-                )
-            for h in range(2):
-                nc.scalar.activation(out=pages[r][:].indirect(listed(h)), in_=d[:, halves[h]], func=COPY, scale=-0.1)
-        m_picked = y_plane[0][:, 0:J]
-        nc.vector.tensor_scalar(
-            out=m_picked, in0=mom32[:].indirect(offsets[:]), scalar1=-0.1, scalar2=0.0, op0=ALU.mult, op1=ALU.add
-        )
-        d_scalar = tile([P, J - SPLIT], F32, "d_scalar")
-        d_vector = y[:, 2 * N - SPLIT // 2 : 2 * N + SPLIT // 2]
-        for d, js in ((d_vector, slice(0, SPLIT)), (d_scalar[:], slice(SPLIT, J))):
-            nc.vector.scalar_tensor_tensor(
-                out=d, in0=acc[3, 0][:, js], scalar=0.03, in1=m_picked[:, js], op0=ALU.mult, op1=ALU.add
-            )
-        nc.vector.tensor_copy(out=pages[3][:].indirect(offsets[:, 0 : SPLIT // 16]), in_=d_vector)
-        nc.scalar.activation(out=pages[3][:].indirect(offsets[:, SPLIT // 16 : J // 16]), in_=d_scalar[:], func=COPY)
+        def entries(js):
+            return offsets[:, js.start // 16 : js.stop // 16]
 
-        for r in range(3):
-            nc.vector.tensor_tensor(out=y_plane[r], in0=m_rows[r], in1=pages[r][:], op=ALU.add)
+        def gather(engine, out, r, js):
+            if engine is nc.scalar:
+                nc.scalar.activation(out=out[:, js], in_=m_rows[r].indirect(entries(js)), func=COPY)
+            else:
+                nc.vector.tensor_copy(out=out[:, js], in_=m_rows[r].indirect(entries(js)))
+
+        def combine(out, r, w, factor, m):
+            nc.vector.scalar_tensor_tensor(out=out, in0=w, scalar=factor, in1=m, op0=ALU.mult, op1=ALU.add)
+
+        def scatter_scalar(r, js, src):
+            nc.scalar.activation(out=pages[r][:].indirect(entries(js)), in_=src, func=COPY, scale=-0.1)
+
+        m_picked = [tile([P, J], F32, f"m_picked{r}") for r in range(PACK)]
+        e = {r: tile([P, J], F32, f"e{r}") for r in (0, 1)}
+        for h in range(2):
+            gather(nc.scalar, m_picked[0], 0, halves[h])
+        for h in range(2):
+            combine(e[0][:, halves[h]], 0, acc[0, halves[h].start][:], -0.3, m_picked[0][:, halves[h]])
+            scatter_scalar(0, halves[h], e[0][:, halves[h]])
+        gather(nc.vector, m_picked[1], 1, slice(0, J))
+        combine(e[1][:], 1, acc[1, 0][:], -0.3, m_picked[1][:])
+        for h in range(2):
+            scatter_scalar(1, halves[h], e[1][:, halves[h]])
+
+        first, rest = slice(0, 128), slice(128, J)
+        e3_first = tile([P, 128], F32, "e3_first")
+        shared = tile([P, 128 + J], F32, "shared")
+        d2, e3_rest = shared[:, 128 : 128 + J], shared[:, 0 : J - 128]
+        gather(nc.vector, m_picked[3], 3, slice(0, J))
+        combine(e3_first[:], 3, acc[3, 0][:, first], -0.3, m_picked[3][:, first])
+        scatter_scalar(3, first, e3_first[:])
+        nc.vector.tensor_scalar(
+            out=m_picked[2][:], in0=mom23[:].indirect(offsets[:]), scalar1=-0.1, scalar2=0.0, op0=ALU.mult, op1=ALU.add
+        )
+        combine(d2, 2, acc[2, 0][:], 0.03, m_picked[2][:])
+        nc.vector.tensor_copy(out=pages[2][:].indirect(listed(0)), in_=d2[:, halves[0]])
+        combine(e3_rest, 3, acc[3, 0][:, rest], -0.3, m_picked[3][:, rest])
+        nc.vector.tensor_copy(out=pages[2][:].indirect(listed(1)), in_=d2[:, halves[1]])
+        scatter_scalar(3, rest, e3_rest)
+
+        for r, engine in ((0, nc.gpsimd), (1, nc.gpsimd), (2, nc.vector)):
+            engine.tensor_tensor(out=y_plane[r], in0=m_rows[r], in1=pages[r][:], op=ALU.add)
             nc.sync.dma_start(y_rows[r], y_plane[r])
-        for cols in (slice(0, CHUNK), slice(CHUNK, 2 * CHUNK), slice(2 * CHUNK, N)):
+        for cols in (slice(0, 256), slice(640, N), slice(256, 640)):
             nc.vector.tensor_tensor(out=y_plane[3][:, cols], in0=m_rows[3][:, cols], in1=pages[3][:, cols], op=ALU.add)
         nc.sync.dma_start(y_rows[3], y_plane[3])
 
         y_scales = tile([P, N], U8, "y_scales")
         words = out_1.rearrange("z p c r -> p (z c r)").bitcast(I32)
-        y_woven = [tile([P, CHUNK, PACK], BF16, f"y_woven{c}") for c in range(N // CHUNK)]
-        for c in (0, 2, 1, 3):
-            cols = slice(c * CHUNK, (c + 1) * CHUNK)
-            dst = y_woven[c][:].rearrange("p (c e) r -> p c r e", e=4)
-            src = y[:].rearrange("p (r n) -> p r n", r=PACK)[:, :, cols].rearrange("p r (c e) -> p c r e", e=4)
-            if c < 2:
-                nc.scalar.copy(out=dst, in_=src)
-            else:
-                nc.vector.tensor_copy(out=dst, in_=src)
-        for c in (0, 2, 1, 3):
-            cols = slice(c * CHUNK, (c + 1) * CHUNK)
-            y_codes = tile([P, CHUNK], U32, f"y_codes{c}")
-            nc.vector.quantize_mx(
-                out=y_codes[:].bitcast(E4M3), scales=y_scales[:, cols], in_=y_woven[c][:].rearrange("p c r -> p (c r)")
+        y_cols = y[:].rearrange("p (r n) -> p r n", r=PACK)
+        chunks = [(0, 256, nc.scalar.copy), (640, N, nc.vector.tensor_copy), (256, 512, nc.scalar.copy), (512, 640, nc.scalar.copy)]
+        y_woven = {}
+        for c0, c1, copy in chunks:
+            y_woven[c0] = tile([P, c1 - c0, PACK], BF16, f"y_woven{c0}")
+            copy(
+                out=y_woven[c0][:].rearrange("p (c e) r -> p c r e", e=4),
+                in_=y_cols[:, :, c0:c1].rearrange("p r (c e) -> p c r e", e=4),
             )
-            nc.sync.dma_start(words[:, cols], y_codes[:].bitcast(I32))
+        for c0, c1, copy in chunks:
+            y_codes = tile([P, c1 - c0], U32, f"y_codes{c0}")
+            nc.vector.quantize_mx(
+                out=y_codes[:].bitcast(E4M3),
+                scales=y_scales[:, c0:c1],
+                in_=y_woven[c0][:].rearrange("p c r -> p (c r)"),
+            )
+            nc.sync.dma_start(words[:, c0:c1], y_codes[:].bitcast(I32))
         scale_rows = out_2.rearrange("z q c -> (z q) c").bitcast(I32)
         for q in range(4):
             queue = nc.scalar if q % 2 == 0 else nc.sync

@@ -35,18 +35,22 @@ def tile_list_sparse_momentum_pl_kernel(tc, xt, g, mom, offs, out_0, out_1, out_
             return sb.tile(shape, dtype, name=name, align_bytes=64)
 
         offsets = sb.tile([P, J // 16], U16, name="offsets")
-        nc.sync.dma_start(offsets[:], offs)
 
         def listed(h):
             return offsets[:, h * LIST_COLS : (h + 1) * LIST_COLS]
 
-        g_rows = g.rearrange("(a p i) n -> a i p n", p=P, i=PACK)
+        g_rows = g.rearrange("(a p i) n -> a p (i n)", p=P, i=PACK)
+        g_loads = [[(0, 1), (1, 2), (2, 4)], [(0, 2), (2, 3), (3, 4)]]
         x_rows = xt.rearrange("(a p i) k -> a p i k", p=P, i=PACK)
         g_raw, x_raw = {}, {}
         for a in range(PASSES):
-            for i in range(PACK):
-                g_raw[a, i] = tile([P, N], F32, f"g_raw{a}{i}")
-                nc.sync.dma_start(g_raw[a, i][:], g_rows[a, i])
+            for i0, i1 in g_loads[a]:
+                rows = tile([P, (i1 - i0) * N], F32, f"g_raw{a}{i0}")
+                nc.sync.dma_start(rows[:], g_rows[a][:, i0 * N : i1 * N])
+                if (a, i0) == (0, 0):
+                    nc.sync.dma_start(offsets[:], offs)
+                for i in range(i0, i1):
+                    g_raw[a, i] = rows[:, (i - i0) * N : (i - i0 + 1) * N]
             x_raw[a] = tile([P, PACK, K], F32, f"x_raw{a}")
             nc.sync.dma_start(x_raw[a][:], x_rows[a])
         mom_rows = mom.rearrange("(p r) n -> r p n", r=PACK)
@@ -67,10 +71,10 @@ def tile_list_sparse_momentum_pl_kernel(tc, xt, g, mom, offs, out_0, out_1, out_
         acc = {(r, js.start): psum.tile([P, js.stop - js.start], F32, name=f"acc{r}_{js.start}") for r, js in sums}
         g_codes, g_scales = {}, {}
         for a in range(PASSES):
-            picked = [tile([P, PACK, HALF], BF16, f"picked{a}{h}") for h in range(2)]
+            picked = [tile([P, PACK, HALF], F32, f"picked{a}{h}") for h in range(2)]
             for i in range(PACK):
-                nc.scalar.activation(out=picked[0][:, i, :], in_=g_raw[a, i][:].indirect(listed(0)), func=COPY)
-                nc.vector.tensor_copy(out=picked[1][:, i, :], in_=g_raw[a, i][:].indirect(listed(1)))
+                nc.scalar.activation(out=picked[0][:, i, :], in_=g_raw[a, i].indirect(listed(0)), func=COPY)
+                nc.vector.tensor_copy(out=picked[1][:, i, :], in_=g_raw[a, i].indirect(listed(1)))
             g_codes[a] = tile([P, J], U32, f"g_codes{a}")
             g_scales[a] = tile([P, J], U8, f"g_scales{a}")
             for h, copy in ((1, nc.vector.tensor_copy), (0, nc.scalar.copy)):

from contextlib import ExitStack

import concourse.mybir as mybir

T, K, N, J = 1024, 512, 1024, 512
FLOPS = 2 * T * K * J

F32 = mybir.dt.float32
BF16 = mybir.dt.bfloat16
U32 = mybir.dt.uint32
I32 = mybir.dt.int32
U16 = mybir.dt.uint16
U8 = mybir.dt.uint8
E4M3 = mybir.dt.float8_e4m3fn_x4
E5M2 = mybir.dt.float8_e5m2_x4
ALU = mybir.AluOpType
COPY = mybir.ActivationFunctionType.Copy

P = 128
PACK = 4
T_PASS = P * PACK
PASSES = T // T_PASS
HALF = J // 2
LIST_COLS = HALF // 16
CHUNK = 256


def tile_list_sparse_momentum_pl_kernel(tc, xt, g, mom, offs, out_0, out_1, out_2):
    nc = tc.nc
    with ExitStack() as ctx:
        sb = ctx.enter_context(tc.tile_pool(name="sb", bufs=1))
        psum = ctx.enter_context(tc.psum_pool(name="psum", bufs=1))

        def tile(shape, dtype, name):
            return sb.tile(shape, dtype, name=name, align_bytes=64)

        offsets = sb.tile([P, J // 16], U16, name="offsets")

        def listed(h):
            return offsets[:, h * LIST_COLS : (h + 1) * LIST_COLS]

        g_rows = g.rearrange("(a p i) n -> a p (i n)", p=P, i=PACK)
        g_loads = [[(0, 1), (1, 2), (2, 4)], [(0, 2), (2, 3), (3, 4)]]
        x_rows = xt.rearrange("(a p i) k -> a p i k", p=P, i=PACK)
        g_raw, x_raw = {}, {}
        for a in range(PASSES):
            for i0, i1 in g_loads[a]:
                rows = tile([P, (i1 - i0) * N], F32, f"g_raw{a}{i0}")
                nc.sync.dma_start(rows[:], g_rows[a][:, i0 * N : i1 * N])
                if (a, i0) == (0, 0):
                    nc.sync.dma_start(offsets[:], offs)
                for i in range(i0, i1):
                    g_raw[a, i] = rows[:, (i - i0) * N : (i - i0 + 1) * N]
            x_raw[a] = tile([P, PACK, K], F32, f"x_raw{a}")
            nc.sync.dma_start(x_raw[a][:], x_rows[a])
        mom_rows = mom.rearrange("(p r) n -> r p n", r=PACK)
        mom0 = tile([P, N], F32, "mom0")
        mom1 = tile([P, N], F32, "mom1")
        mom23 = tile([P, 2 * N], F32, "mom23")
        m_rows = [mom0[:], mom1[:], mom23[:, 0:N], mom23[:, N : 2 * N]]
        for r in range(2):
            nc.sync.dma_start(m_rows[r], mom_rows[r])
        nc.sync.dma_start(mom23[:], mom.rearrange("(p u e) n -> u p (e n)", u=2, e=2)[1])

        pages = [tile([P, N], F32, f"page{r}") for r in range(PACK)]
        for r in range(PACK):
            nc.gpsimd.memset(pages[r][:], 0.0)

        halves = [slice(h * HALF, (h + 1) * HALF) for h in range(2)]
        sums = [(0, halves[0]), (0, halves[1])] + [(r, slice(0, J)) for r in range(1, PACK)]
        acc = {(r, js.start): psum.tile([P, js.stop - js.start], F32, name=f"acc{r}_{js.start}") for r, js in sums}
        g_codes, g_scales = {}, {}
        for a in range(PASSES):
            picked = [tile([P, PACK, HALF], F32, f"picked{a}{h}") for h in range(2)]
            for i in range(PACK):
                nc.scalar.activation(out=picked[0][:, i, :], in_=g_raw[a, i].indirect(listed(0)), func=COPY)
                nc.vector.tensor_copy(out=picked[1][:, i, :], in_=g_raw[a, i].indirect(listed(1)))
            g_codes[a] = tile([P, J], U32, f"g_codes{a}")
            g_scales[a] = tile([P, J], U8, f"g_scales{a}")
            for h, copy in ((1, nc.vector.tensor_copy), (0, nc.scalar.copy)):
                woven = tile([P, HALF, PACK], BF16, f"g_woven{a}{h}")
                copy(
                    out=woven[:].rearrange("p (c e) i -> p c i e", e=4),
                    in_=picked[h][:].rearrange("p i (c e) -> p c i e", e=4),
                )
                nc.vector.quantize_mx(
                    out=g_codes[a][:, halves[h]].bitcast(E5M2),
                    scales=g_scales[a][:, halves[h]],
                    in_=woven[:].rearrange("p c i -> p (c i)"),
                )
            for q in range(2):
                woven = tile([P, 2, P, PACK], BF16, f"x_woven{a}{q}")
                for ms, copy in ((slice(0, P // 2), nc.vector.tensor_copy), (slice(P // 2, P), nc.scalar.copy)):
                    copy(
                        out=woven[:, :, ms, :].rearrange("p s m i -> p m i s"),
                        in_=x_raw[a][:].rearrange("p i (m r) -> p m i r", r=PACK)[:, ms, :, 2 * q : 2 * q + 2],
                    )
                for s in range(2):
                    r = 2 * q + s
                    codes = tile([P, P], U32, f"x_codes{a}{r}")
                    scales = tile([P, P], U8, f"x_scales{a}{r}")
                    nc.vector.quantize_mx(
                        out=codes[:].bitcast(E4M3),
                        scales=scales[:],
                        in_=woven[:, s, :, :].rearrange("p m i -> p (m i)"),
                    )
                    for js in [js for plane, js in sums if plane == r]:
                        nc.tensor.matmul_mx(
                            out=acc[r, js.start][:],
                            lhsT=codes[:].bitcast(E4M3),
                            lhsT_scale=scales[:],
                            rhs=g_codes[a][:, js].bitcast(E5M2),
                            rhs_scale=g_scales[a][:, js],
                            start=(a == 0),
                            stop=(a == PASSES - 1),
                        )

        y = tile([P, PACK * N], F32, "y")
        y_plane = [y[:, r * N : (r + 1) * N] for r in range(PACK)]
        y_rows = out_0.rearrange("(p r) n -> r p n", r=PACK)
        def entries(js):
            return offsets[:, js.start // 16 : js.stop // 16]

        def gather(engine, out, r, js):
            if engine is nc.scalar:
                nc.scalar.activation(out=out[:, js], in_=m_rows[r].indirect(entries(js)), func=COPY)
            else:
                nc.vector.tensor_copy(out=out[:, js], in_=m_rows[r].indirect(entries(js)))

        def combine(out, r, w, factor, m):
            nc.vector.scalar_tensor_tensor(out=out, in0=w, scalar=factor, in1=m, op0=ALU.mult, op1=ALU.add)

        def scatter_scalar(r, js, src):
            nc.scalar.activation(out=pages[r][:].indirect(entries(js)), in_=src, func=COPY, scale=-0.1)

        m_picked = [tile([P, J], F32, f"m_picked{r}") for r in range(PACK)]
        e = {r: tile([P, J], F32, f"e{r}") for r in (0, 1)}
        for h in range(2):
            gather(nc.scalar, m_picked[0], 0, halves[h])
        for h in range(2):
            combine(e[0][:, halves[h]], 0, acc[0, halves[h].start][:], -0.3, m_picked[0][:, halves[h]])
            scatter_scalar(0, halves[h], e[0][:, halves[h]])
        gather(nc.vector, m_picked[1], 1, slice(0, J))
        combine(e[1][:], 1, acc[1, 0][:], -0.3, m_picked[1][:])
        for h in range(2):
            scatter_scalar(1, halves[h], e[1][:, halves[h]])

        first, rest = slice(0, 128), slice(128, J)
        e3_first = tile([P, 128], F32, "e3_first")
        shared = tile([P, 128 + J], F32, "shared")
        d2, e3_rest = shared[:, 128 : 128 + J], shared[:, 0 : J - 128]
        gather(nc.vector, m_picked[3], 3, slice(0, J))
        combine(e3_first[:], 3, acc[3, 0][:, first], -0.3, m_picked[3][:, first])
        scatter_scalar(3, first, e3_first[:])
        nc.vector.tensor_scalar(
            out=m_picked[2][:], in0=mom23[:].indirect(offsets[:]), scalar1=-0.1, scalar2=0.0, op0=ALU.mult, op1=ALU.add
        )
        combine(d2, 2, acc[2, 0][:], 0.03, m_picked[2][:])
        nc.vector.tensor_copy(out=pages[2][:].indirect(listed(0)), in_=d2[:, halves[0]])
        combine(e3_rest, 3, acc[3, 0][:, rest], -0.3, m_picked[3][:, rest])
        nc.vector.tensor_copy(out=pages[2][:].indirect(listed(1)), in_=d2[:, halves[1]])
        scatter_scalar(3, rest, e3_rest)

        for r, engine in ((0, nc.gpsimd), (1, nc.gpsimd), (2, nc.vector)):
            engine.tensor_tensor(out=y_plane[r], in0=m_rows[r], in1=pages[r][:], op=ALU.add)
            nc.sync.dma_start(y_rows[r], y_plane[r])
        for cols in (slice(0, 256), slice(640, N), slice(256, 640)):
            nc.vector.tensor_tensor(out=y_plane[3][:, cols], in0=m_rows[3][:, cols], in1=pages[3][:, cols], op=ALU.add)
        nc.sync.dma_start(y_rows[3], y_plane[3])

        y_scales = tile([P, N], U8, "y_scales")
        words = out_1.rearrange("z p c r -> p (z c r)").bitcast(I32)
        y_cols = y[:].rearrange("p (r n) -> p r n", r=PACK)
        chunks = [(0, 256, nc.scalar.copy), (640, N, nc.vector.tensor_copy), (256, 512, nc.scalar.copy), (512, 640, nc.scalar.copy)]
        y_woven = {}
        for c0, c1, copy in chunks:
            y_woven[c0] = tile([P, c1 - c0, PACK], BF16, f"y_woven{c0}")
            copy(
                out=y_woven[c0][:].rearrange("p (c e) r -> p c r e", e=4),
                in_=y_cols[:, :, c0:c1].rearrange("p r (c e) -> p c r e", e=4),
            )
        for c0, c1, copy in chunks:
            y_codes = tile([P, c1 - c0], U32, f"y_codes{c0}")
            nc.vector.quantize_mx(
                out=y_codes[:].bitcast(E4M3),
                scales=y_scales[:, c0:c1],
                in_=y_woven[c0][:].rearrange("p c r -> p (c r)"),
            )
            nc.sync.dma_start(words[:, c0:c1], y_codes[:].bitcast(I32))
        scale_rows = out_2.rearrange("z q c -> (z q) c").bitcast(I32)
        for q in range(4):
            queue = nc.scalar if q % 2 == 0 else nc.sync
            queue.dma_start(scale_rows[4 * q : 4 * q + 4, :], y_scales[32 * q : 32 * q + 4, :].bitcast(I32))
